import numpy as np, ml_dtypes
CORES = [3,7,11,15,131,135,139,143]
N = 8
import mx_ref
BF = ml_dtypes.bfloat16
def entries(a):
    return np.ascontiguousarray(a.T).reshape(-1)
def table(e):
    return np.ascontiguousarray(np.reshape(e, (-1, 16)).T).astype(np.int32)
def cols(t, e):
    v = np.concatenate([t.reshape(128, -1, 4), np.zeros((128, 1, 4), BF)], axis=1)
    return np.ascontiguousarray(v[:, e]).reshape(128, -1)
def cut(t, i, w=512):
    return t[:, w * i:w * i + w]
def f(rng, *shape):
    return mx_ref.flush((rng.standard_normal(shape, dtype=np.float32) * np.exp2(rng.integers(-2, 3, shape[:-1] + (1,)))).astype(BF))
def wide(rng, *shape, cols=0):
    v = rng.standard_normal(shape, dtype=np.float32) * np.exp2(rng.integers(-12, 13, shape)).astype(np.float32)
    if cols: v *= np.repeat(np.exp2(rng.integers(-cols, cols + 1, shape[:-2] + (1, shape[-1] // 4))) * (rng.random(shape[:-2] + (1, shape[-1] // 4)) > 0.0625), 4, axis=-1).astype(np.float32)
    return mx_ref.flush(v.astype(BF))
T, CAPP, F = 128, 80, 8
def inverse(e):
    o = np.full(F * T, -1)
    k = np.flatnonzero(e >= 0); k = k[np.argsort(e[k], kind="stable")]; v = e[k]
    at = np.arange(len(k)) - np.searchsorted(v, v); keep = at < F
    o[(F * v + at)[keep]] = k[keep]
    return o
def counts(rng, most=CAPP):
    n = np.zeros((N, N), int)
    for r in range(N):
        a = rng.integers(T // N, 4 * T // N + 1, N)
        n[:, r] = a + np.bincount(rng.permutation(np.repeat(np.arange(N), most - a))[:4 * T - a.sum()], minlength=N)
    return n
def senders(rng, n):
    return np.stack([rng.permutation(np.repeat(np.arange(N), n[:, r])) for r in range(N)])
def lists(rng, A, node=None, top=None, popular=False, big=None):
    sn = np.full((N, N * CAPP), -1); nb = np.zeros((N, 4 * T), int)
    for s in range(N):
        d, e = np.nonzero(A == s); free = rng.permutation(T)
        if node is not None: v = node[d, e]
        elif top is not None:
            t = top[d, e]; h = (t.sum() + F - 1) // F; v = np.zeros(len(d), int); big.append(free[:h])
            v[t] = rng.permutation(np.repeat(free[:h], F))[:t.sum()]
            v[~t] = rng.permutation(np.repeat(free[h:], F))[:(~t).sum()]
        else:
            h = len(d) // 16 if popular else 0
            v = rng.permutation(np.concatenate([np.repeat(free[:h], F), rng.permutation(np.repeat(free[h:], F))[:len(d) - F * h]]))
        for q in range(N):
            k = np.flatnonzero(d == q); c = rng.permutation(CAPP)[:len(k)]
            sn[s, q * CAPP + c] = v[k]; nb[q, e[k]] = s * CAPP + c
    return {"sn": np.stack([table(a) for a in sn]), "nb": np.stack([table(a) for a in nb]), "il": np.stack([table(inverse(a)) for a in sn])}
def setup_inputs(rng):
    return {"x": f(rng, N, 128, 4 * T), "gr": f(rng, N, 128, 4 * T), "w": np.repeat(f(rng, 1, 128, 2048), N, axis=0), "w2": np.repeat(f(rng, 1, 128, 2048), N, axis=0), **lists(rng, senders(rng, counts(rng)))}
def setup_inputs_ties(rng):
    d = setup_inputs(rng); own = d["x"].reshape(N, 128, T, 4)
    d["x"] = np.ascontiguousarray(np.where(rng.random((N, 1, T, 1)) < 0.7, own[:1], own)).reshape(N, 128, 4 * T)
    n = counts(rng, min(CAPP, T)); A = np.zeros((N, 4 * T), int); node = np.zeros((N, 4 * T), int)
    e = np.arange(4 * T); j = e % T; k = (e // T + j) % 4
    for r in range(N):
        o = rng.permutation(N); to = 4 * rng.permutation(T)[j] + k
        A[r, to] = np.repeat(o, n[o, r]); node[r, to] = rng.permutation(T)[j]
    return {**d, **lists(rng, A, node=node)}
def setup_inputs_oneside(rng):
    d = setup_inputs(rng); top = np.zeros((N, 4 * T), bool); big = []
    for r in range(N): top[r, 4 * rng.permutation(T)[:T // 2] + 3] = True
    d.update(lists(rng, senders(rng, counts(rng)), top=top, big=big))
    v = np.abs(d["x"].astype(np.float32)).reshape(N, 128, T, 4)
    for s in range(N): v[s][:, big[s]] *= 64
    d["x"] = v.reshape(N, 128, 4 * T).astype(BF); d["w"] = np.abs(d["w"].astype(np.float32)).astype(BF)
    return d
def setup_inputs_popular(rng):
    return {**setup_inputs(rng), **lists(rng, senders(rng, counts(rng)), popular=True)}
def setup_inputs_full(rng):
    n = np.zeros((N, N), int); o = rng.permutation(N); at = rng.permutation(N)
    m = 4 * T // CAPP; rest = 4 * T - m * CAPP
    for r in range(N):
        for j in range(m): n[o[(at[r] + j) % N], r] = CAPP
        if rest: n[o[(at[r] + m) % N], r] = rest
    return {**setup_inputs(rng), **lists(rng, senders(rng, n))}
def setup_inputs_spread(rng):
    d = setup_inputs(rng); d["x"] = wide(rng, N, 128, 4 * T, cols=8); return d
def check_inputs(d):
    b = []
    for t in ("w", "w2"):
        if (d[t] != d[t][:1]).any(): b.append(t)
    e = np.stack([entries(a) for a in d["sn"]])
    if e.min() < -1 or e.max() >= T: b.append("sn")
    e = np.clip(e, -1, T - 1)
    for r in range(N):
        if np.bincount(e[r][e[r] >= 0], minlength=T).max() > F: b.append("sn")
        if not np.array_equal(np.sort(entries(d["nb"][r])), np.flatnonzero(e[:, r * CAPP:(r + 1) * CAPP].reshape(-1) >= 0)): b.append("nb")
        if not np.array_equal(entries(d["il"][r]), inverse(e[r])): b.append("il")
    return b
def four(v):
    return [mx_ref.quantize(np.ascontiguousarray(cut(v, b))) for b in range(4)]
def reference(x, gr, w, w2, sn, nb, il):
    G = []
    for r in range(N):
        arrived = mx_ref.quantize(np.concatenate([cols(x[s], entries(sn[s])[r * CAPP:(r + 1) * CAPP]) for s in range(N)], axis=1))
        e = entries(nb[r])
        z = [mx_ref.matmul(W, arrived)[:, e].reshape(128, T, 4) + np.float32(0.0) for W in four(w[r])]
        win = np.stack([v.argmax(axis=2) for v in z], axis=2)
        g = gr[r].reshape(128, T, 4); back = np.zeros((128, N * CAPP, 4), BF)
        for k in range(4): back[:, e[k::4]] = np.where(win == k, g, np.zeros_like(g))
        G.append(back)
    y = np.zeros((N, 128, 4 * T), np.float32)
    for s in range(N):
        q = mx_ref.quantize(np.concatenate([G[r][:, s * CAPP:(s + 1) * CAPP].reshape(128, -1) for r in range(N)], axis=1))
        e = entries(il[s])
        for b, V in enumerate(four(w2[s])):
            u = mx_ref.matmul(V, q); t = np.zeros((128, T), np.float32)
            for i in range(F):
                k = e[i::F]; has = k >= 0
                t[:, has] += u[:, k[has]]
            y[s][:, T * b:T * b + T] = t
    return {"y": y}

@@ -1,0 +1,378 @@
+from concourse.bass import DstId, RemoteDMATransfer
+from concourse.mybir import dt, AluOpType, ActivationFunctionType
+
+NR, NODES, CAPP, F = 8, 128, 80, 8
+SLOTS = NR * CAPP
+PAD = 8
+BIG = 1e29
+POS = (1, 3, 7, 5)
+
+SCRATCH = {
+    "xs": ("sbuf", [128, 4 * NODES], "bfloat16"),
+    "grs": ("sbuf", [128, 4 * NODES], "bfloat16"),
+    "ws": ("sbuf", [128, 2048], "bfloat16"),
+    "ws2": ("sbuf", [128, 2048], "bfloat16"),
+    "snt": ("sbuf", [128, SLOTS // 16], "int32"),
+    "nbt": ("sbuf", [128, 4 * NODES // 16], "int32"),
+    "ilt": ("sbuf", [128, F * NODES // 16], "int32"),
+    "xg": ("sbuf", [128, 4 * SLOTS], "bfloat16"),
+    "xq": ("sbuf", [128, SLOTS], "float8_e4m3fn_x4"),
+    "xp": ("sbuf", [128, SLOTS], "uint8"),
+    "wq": ("sbuf", [128, 512], "float8_e4m3fn_x4"),
+    "wp": ("sbuf", [128, 512], "uint8"),
+    "vq": ("sbuf", [128, 512], "float8_e4m3fn_x4"),
+    "vp": ("sbuf", [128, 512], "uint8"),
+    "landq": ("sbuf", [128, SLOTS], "float8_e4m3fn_x4"),
+    "landp": ("sbuf", [128, SLOTS], "uint8"),
+    "backq": ("sbuf", [128, SLOTS], "float8_e4m3fn_x4"),
+    "backp": ("sbuf", [128, SLOTS], "uint8"),
+    "gs": ("sbuf", [128, 4 * SLOTS], "bfloat16"),
+    "gq": ("sbuf", [128, SLOTS], "float8_e4m3fn_x4"),
+    "gp": ("sbuf", [128, SLOTS], "uint8"),
+    "ps": ("psum", [128, 4096], "float32"),
+    "nbl": ("sbuf", [128, 32], "uint16"),
+    "nbm": ("sbuf", [128, 32], "int32"),
+    "nbs": ("sbuf", [128, 32], "int32"),
+    "scl": ("sbuf", [128, 32], "uint16"),
+    "pix": ("sbuf", [128, 1], "int32"),
+    "pib": ("sbuf", [128, 1], "int32"),
+    "sh": ("sbuf", [128, 1], "float32"),
+    "vals": ("sbuf", [128, 512], "float32"),
+    "win": ("sbuf", [128, 2 * SLOTS], "float32"),
+    "wint": ("sbuf", [128, 2 * SLOTS], "float32"),
+    "invf": ("sbuf", [128, 40], "float32"),
+    "inv": ("sbuf", [128, 40], "uint16"),
+    "ill": ("sbuf", [128, 64], "uint16"),
+    "mpat": ("sbuf", [128, 512], "float32"),
+    "spat": ("sbuf", [128, 512], "float32"),
+    "yt": ("sbuf", [128, 512], "float32"),
+}
+for _i in range(4):
+    SCRATCH["off%d" % _i] = ("sbuf", [128, 40], "uint16")
+    SCRATCH["z%d" % _i] = ("sbuf", [128, SLOTS], "float32")
+    SCRATCH["zg%d" % _i] = ("sbuf", [128, 512], "float32")
+    SCRATCH["pm%d" % _i] = ("sbuf", [128, 512], "float32")
+    SCRATCH["grx%d" % _i] = ("sbuf", [128, 1024], "bfloat16")
+    SCRATCH["tb%d" % _i] = ("sbuf", [128, 1024], "bfloat16")
+    SCRATCH["u%d" % _i] = ("sbuf", [128, PAD + SLOTS], "float32")
+for _i in range(2):
+    SCRATCH["msk%d" % _i] = ("sbuf", [128, 1024], "bfloat16")
+for _i in range(8):
+    SCRATCH["ug%d" % _i] = ("sbuf", [128, 512], "float32")
+    SCRATCH["us%d" % _i] = ("sbuf", [128, 512], "float32")
+
+SEMAPHORES = ["sv", "ss", "st", "sg", "dsn", "dx", "dw", "dnb", "dgr", "dw2", "dil", "own1", "own2", "dy",
+              "aO", "aH", "bO", "bH", "ls"]
+
+
+def rank_program(g, core, T, topo):
+    rank = T.rank_of(core)
+    if rank is None:
+        return
+    A, COPY = AluOpType, ActivationFunctionType.Copy
+    V, S, P, Y = g.vector, g.scalar, g.tensor, g.sync
+    queue = {"v": V, "s": S, "t": P, "g": g, "y": Y}
+    sem_of = {"v": "sv", "s": "ss", "t": "st", "g": "sg"}
+    count = {"v": 0, "s": 0, "t": 0, "g": 0}
+    seen = {}
+
+    def done(e, ins):
+        ins.then_inc(T.sem[sem_of[e]], 1)
+        count[e] += 1
+        return (sem_of[e], count[e])
+
+    def need(e, *tokens):
+        for name, val in tokens:
+            if seen.get((e, name), 0) < val:
+                queue[e].wait_ge(T.sem[name], val)
+                seen[(e, name)] = val
+
+    cores = list(T.cores)
+    other = [d for d in range(NR) if topo.host(cores[d]) != topo.host(core)]
+    here = [d for d in range(NR) if topo.host(cores[d]) == topo.host(core)]
+    o0, h0 = other[0] * CAPP, here[0] * CAPP
+    half = len(other) * CAPP
+    engines = {}
+    for i, d in enumerate(other):
+        e = topo.engines(core, cores[d])
+        per = len(e) // len(other)
+        engines[d] = e[i * per:(i + 1) * per]
+    chip_peer = [d for d in here if d != rank and cores[d] in topo.cores_of(core)]
+    mates = [d for d in here if d != rank and d not in chip_peer]
+    off = topo.engines(core, cores[mates[0]])
+    per = len(off) // len(mates)
+    for i, d in enumerate(mates):
+        engines[d] = off[i * per:(i + 1) * per]
+    for d in chip_peer:
+        engines[d] = [e for e in topo.engines(core, cores[d]) if e not in off][:per]
+    near = chip_peer + mates
+    inc_o = 2 * sum(len(engines[d]) for d in other)
+    inc_h = 2 * sum(len(engines[d]) for d in near)
+
+    def send(dests, sq, sp, dq, dp, sem):
+        for src, dst, codes in ((sq, dq, True), (sp, dp, False)):
+            tr = []
+            for d in dests:
+                rid, pid = topo.addr(cores[d], core)
+                a = T[src][:, d * CAPP:(d + 1) * CAPP]
+                b = T[dst][:, rank * CAPP:(rank + 1) * CAPP]
+                if codes:
+                    a, b = a.bitcast(dt.uint8), b.bitcast(dt.uint8)
+                tr.append(RemoteDMATransfer(dst_ids=[DstId(rid=rid, pnc=pid)],
+                                            dma_engine_mask=sum(1 << e for e in engines[d]),
+                                            remote_sem=T.sem[sem], src=a, dst=b))
+            g.remote_dma_fused(tr, local_sem=T.sem.ls)
+
+    def keep(sq, sp, dq, dp, sem):
+        a, b = rank * CAPP, (rank + 1) * CAPP
+        Y.dma_start(out=T[dq][:, a:b].bitcast(dt.uint8), in_=T[sq][:, a:b].bitcast(dt.uint8)).then_inc(T.sem[sem], 16)
+        Y.dma_start(out=T[dp][:, a:b], in_=T[sp][:, a:b]).then_inc(T.sem[sem], 16)
+
+    Y.dma_start(out=T.xs[:], in_=T.x[:]).then_inc(T.sem.dx, 16)
+    for k in range(4):
+        S.dma_start(out=T.snt[16 * k:16 * k + 16, :], in_=T.sn[:, :]).then_inc(T.sem.dsn, 16)
+    for k in range(4, 8):
+        Y.dma_start(out=T.snt[16 * k:16 * k + 16, :], in_=T.sn[:, :]).then_inc(T.sem.dsn, 16)
+    S.dma_start(out=T.ws[:], in_=T.w[:]).then_inc(T.sem.dw, 16)
+    for k in range(8):
+        Y.dma_start(out=T.nbt[16 * k:16 * k + 16, :], in_=T.nb[:, :]).then_inc(T.sem.dnb, 16)
+    Y.dma_start(out=T.grs[:], in_=T.gr[:]).then_inc(T.sem.dgr, 16)
+    Y.dma_start(out=T.ws2[:], in_=T.w2[:]).then_inc(T.sem.dw2, 16)
+    for k in range(8):
+        Y.dma_start(out=T.ilt[16 * k:16 * k + 16, :], in_=T.il[:, :]).then_inc(T.sem.dil, 16)
+
+    pix = done("g", g.iota(T.pix[:], [[0, 1]], 0, 1))
+    for k in range(4):
+        vals = done("g", g.iota(T.vals[:, k:512:4], [[8, 128]], POS[k], 0, allow_small_or_imprecise_dtypes=True))
+    mk = [None, None]
+    mk[0] = done("g", g.iota(T.msk0[:, 0:1024:2], [[0, 256], [-1, 2]], 0, 0, allow_small_or_imprecise_dtypes=True))
+
+    t0 = done("v", V.memset(T.mpat[:], BIG))
+    grz = [None] * 4
+    for b in (2, 3):
+        need("s", t0)
+        grz[b] = done("s", S.activation(T["grx%d" % b][:, 1:1024:2], T.mpat[:], COPY, scale=0.0))
+    win = done("v", V.memset(T.win[:], 0.0))
+    for b in (0, 1):
+        grz[b] = done("v", V.memset(T["grx%d" % b][:, 1:1024:2], 0.0))
+    need("v", t0, *[grz[b] for b in (2, 3)])
+    mpat = done("v", V.memset(T.mpat[:, 0:512:4], -BIG))
+
+    need("v", ("dsn", 128))
+    offs = {}
+    for t in (2, 0, 1, 3):
+        offs[t] = done("v", V.tensor_scalar(T["off%d" % t][:], T.snt[:], 4.0, float(t), A.mult, A.add))
+    for e in ("v", "s"):
+        need(e, ("dx", 16))
+    n16 = half // 16
+
+    def gather_x(a):
+        toks = []
+        for e, t in (("v", 0), ("s", 2), ("v", 1), ("s", 3)):
+            need(e, offs[t])
+            src = T.xs[:, :].indirect(T["off%d" % t][:, a // 16:a // 16 + n16])
+            dst = T.xg[:, 4 * a + t:4 * (a + half):4]
+            toks.append(done(e, V.tensor_copy(dst, src) if e == "v" else S.activation(dst, src, COPY)))
+        return toks
+
+    def quantise(q, p, t, a, n):
+        return done("v", V.quantize_mx(T[q][:, a:a + n], T[p][:, a:a + n], T[t][:, 4 * a:4 * (a + n)]))
+
+    need("v", *gather_x(o0))
+    tok = quantise("xq", "xp", "xg", o0, half)
+    need("g", tok)
+    send(other, "xq", "xp", "landq", "landp", "aO")
+    need("v", *gather_x(h0))
+    tok = quantise("xq", "xp", "xg", h0, half)
+    need("g", tok)
+    send(near, "xq", "xp", "landq", "landp", "aH")
+    need("y", tok)
+    keep("xq", "xp", "landq", "landp", "own1")
+    mk[1] = done("g", g.iota(T.msk1[:, 0:1024:2], [[0, 256], [-1, 2]], 0, 0, allow_small_or_imprecise_dtypes=True))
+
+    need("v", ("dw", 16))
+    wq = quantise("wq", "wp", "ws", 0, 512)
+    need("v", ("dnb", 128), pix)
+    a1 = done("v", V.tensor_scalar(T.pib[:], T.pix[:], 16, None, A.bitwise_and))
+    a2 = done("v", V.tensor_scalar(T.nbm[:], T.nbt[:], 1008, None, A.bitwise_and))
+    nbl = done("v", V.tensor_copy(T.nbl[:], T.nbt[:]))
+    need("v", a1)
+    a3 = done("v", V.tensor_copy(T.sh[:], T.pib[:]))
+    need("v", a2)
+    a4 = done("v", V.tensor_tensor(T.nbs[:], T.nbm[:], T.nbt[:], A.add))
+    need("v", a3, a4)
+    a5 = done("v", V.tensor_scalar(T.scl[:], T.nbs[:], T.sh[:], None, A.add))
+    need("v", a5, vals, win)
+    a6 = done("v", V.tensor_copy(T.win[:].indirect(T.scl[:]), T.vals[:]))
+    need("v", a6)
+    a7 = done("v", V.transpose(T.wint[:], T.win[:]))
+    need("v", a7)
+    a8 = done("v", V.tensor_tensor(T.invf[:], T.wint[:, 0:1280:32], T.wint[:, 16:1280:32], A.add))
+    need("v", a8)
+    inv = done("v", V.tensor_copy(T.inv[:], T.invf[:]))
+
+    need("s", ("dgr", 16))
+    grx = [None] * 4
+    for b in range(4):
+        for k in range(4):
+            grx[b] = done("s", S.activation(T["grx%d" % b][:, 2 * k:1024:8], T.grs[:, b:512:4], COPY))
+
+    def products(stat, plane, rq, rp, a, bank, free):
+        toks = []
+        for b in range(4):
+            need("t", *free[b])
+            toks.append(done("t", P.matmul_mx(T.ps[:, 512 * (bank + b):512 * (bank + b) + half],
+                                              T[stat][:, 128 * b:128 * b + 128], T[plane][:, 128 * b:128 * b + 128],
+                                              T[rq][:, a:a + half], T[rp][:, a:a + half], True, True)))
+        return toks
+
+    def unload(e, name, b, a, shift, bank, tok):
+        need(e, tok)
+        dst = T["%s%d" % (name, b)][:, shift + a:shift + a + half]
+        src = T.ps[:, 512 * (bank + b):512 * (bank + b) + half]
+        return done(e, V.tensor_copy(dst, src) if e == "v" else S.activation(dst, src, COPY))
+
+    none = [()] * 4
+    need("t", wq, ("aO", inc_o))
+    pt = products("wq", "wp", "landq", "landp", o0, 0, none)
+    zo = [None] * 4
+    for b in range(4):
+        zo[b] = unload("s" if b % 2 else "v", "z", b, o0, 0, 0, pt[b])
+    need("t", ("aH", inc_h), ("own1", 32))
+    pt = products("wq", "wp", "landq", "landp", h0, 4, none)
+    zh = [None] * 4
+    for b in (0, 1, 2, 3):
+        zh[b] = unload("s" if b == 1 else "v", "z", b, h0, 0, 4, pt[b])
+
+    zg, sg = [None] * 4, {}
+
+    def order_z(b):
+        need("s", zo[b], zh[b], nbl)
+        zg[b] = done("s", S.activation(T["zg%d" % b][:], T["z%d" % b][:].indirect(T.nbl[:]), COPY))
+
+    def slots(e, b, a, n):
+        need(e, inv, chain[b])
+        dst = T.gs[:, 4 * a + b:4 * (a + n):4]
+        src = T["tb%d" % b][:].indirect(T.inv[:, a // 16:(a + n) // 16])
+        return done(e, V.tensor_copy(dst, src) if e == "v" else S.activation(dst, src, COPY))
+
+    pm, cm, chain = [None] * 4, [None] * 4, [None] * 4
+
+    def running(b):
+        need("v", zg[b], mpat)
+        pm[b] = done("v", V.tensor_tensor_scan(T["pm%d" % b][:], T.mpat[:], T["zg%d" % b][:], 0.0, A.min, A.max))
+
+    def compare(b):
+        need("v", pm[b], mk[b % 2])
+        m, k = T["pm%d" % b], T["msk%d" % (b % 2)]
+        cm[b] = done("v", V.tensor_tensor(k[:, 3:1024:8], m[:, 1:512:4], m[:, 3:512:4], A.is_ge))
+        done("v", V.tensor_tensor(k[:, 1:1024:8], m[:, 0:512:4], m[:, 3:512:4], A.is_ge))
+        done("v", V.tensor_tensor(k[:, 5:1024:8], m[:, 2:512:4], m[:, 3:512:4], A.is_lt))
+        need("v", cm[b])
+        cm[b] = done("v", V.tensor_scalar(k[:, 7:1024:8], k[:, 3:1024:8], -1.0, 1.0, A.mult, A.add))
+
+    def masked(b):
+        need("v", cm[b], grx[b], grz[b])
+        chain[b] = done("v", V.tensor_tensor_scan(T["tb%d" % b][:], T["msk%d" % (b % 2)][:], T["grx%d" % b][:], 0.0, A.mult, A.add))
+
+    order_z(0)
+    order_z(1)
+    running(0)
+    compare(0)
+    running(1)
+    masked(0)
+    order_z(2)
+    slots0 = slots("s", 0, 0, SLOTS)
+    compare(1)
+    running(2)
+    masked(1)
+    order_z(3)
+    slots1 = slots("s", 1, 0, SLOTS)
+    compare(2)
+    running(3)
+    masked(2)
+    slots2 = slots("s", 2, 0, SLOTS)
+    compare(3)
+    masked(3)
+    q1 = slots("v", 3, o0, half // 2)
+    q2 = slots("s", 3, o0 + half // 2, half // 2)
+    q3 = slots("s", 3, h0, half)
+    need("v", q1, slots0, slots1, slots2, q2)
+    tok = quantise("gq", "gp", "gs", o0, half)
+    need("g", tok)
+    send(other, "gq", "gp", "backq", "backp", "bO")
+    need("v", q3)
+    tok = quantise("gq", "gp", "gs", h0, half)
+    need("g", tok)
+    send(near, "gq", "gp", "backq", "backp", "bH")
+    need("y", tok)
+    keep("gq", "gp", "backq", "backp", "own2")
+
+    need("v", ("dw2", 16))
+    vq = quantise("vq", "vp", "ws2", 0, 512)
+    need("v", ("dil", 128))
+    ill = done("v", V.tensor_scalar(T.ill[:], T.ilt[:], float(PAD), None, A.add))
+    zpad = [done("v", V.memset(T["u%d" % b][:, 0:PAD], 0.0)) for b in range(4)]
+    c1 = done("v", V.memset(T.spat[:], 1.0))
+    need("v", c1)
+    spat = done("v", V.memset(T.spat[:, 0:512:8], 0.0))
+
+    need("t", vq, ("bO", inc_o))
+    pt = products("vq", "vp", "backq", "backp", o0, 0, [(zo[b],) for b in range(4)])
+    uo = [None] * 4
+    for b in range(4):
+        uo[b] = unload("s" if b % 2 else "v", "u", b, o0, PAD, 0, pt[b])
+    need("t", ("bH", inc_h), ("own2", 32))
+    pt = products("vq", "vp", "backq", "backp", h0, 4, [(zh[b],) for b in range(4)])
+    uh = [None] * 4
+    for b in range(4):
+        uh[b] = unload("s" if b == 1 else "v", "u", b, h0, PAD, 4, pt[b])
+
+    ug, us, yt = [None] * 8, [None] * 8, [None] * 8
+
+    def take(e, i):
+        b, h = i // 2, i % 2
+        need(e, uo[b], uh[b], zpad[b], ill)
+        src = T["u%d" % b][:].indirect(T.ill[:, 32 * h:32 * h + 32])
+        dst = T["ug%d" % i][:]
+        ug[i] = done(e, V.tensor_copy(dst, src) if e == "v" else S.activation(dst, src, COPY))
+
+    def add_up(i):
+        need("v", ug[i], spat)
+        us[i] = done("v", V.tensor_tensor_scan(T["us%d" % i][:], T.spat[:], T["ug%d" % i][:], 0.0, A.mult, A.add))
+
+    def pick(i):
+        need("v", us[i])
+        yt[i] = done("v", V.tensor_copy(T.yt[:, 64 * i:64 * i + 64], T["us%d" % i][:, 7:512:8]))
+
+    def store(b):
+        need("y", yt[2 * b], yt[2 * b + 1])
+        Y.dma_start(out=T.y[:, 128 * b:128 * b + 128], in_=T.yt[:, 128 * b:128 * b + 128]).then_inc(T.sem.dy, 16)
+
+    for i in range(7):
+        take("s", i)
+    add_up(0)
+    add_up(1)
+    pick(0)
+    pick(1)
+    add_up(2)
+    store(0)
+    take("v", 7)
+    add_up(3)
+    pick(2)
+    pick(3)
+    store(1)
+    add_up(4)
+    add_up(5)
+    pick(4)
+    pick(5)
+    store(2)
+    add_up(7)
+    add_up(6)
+    pick(7)
+    pick(6)
+    store(3)
+
+    Y.wait_ge(T.sem.dy, 64)
+    need("g", ("sv", count["v"]), ("ss", count["s"]), ("st", count["t"]), ("sg", count["g"]))
+    g.wait_ge(T.sem.ls, 2 * (inc_o + inc_h))

@@ -3,17 +3,21 @@ from concourse.mybir import dt, AluOpType, ActivationFunctionType
 
 NR, NODES, CAPP, F = 8, 128, 80, 8
 SLOTS = NR * CAPP
+PAIR = 2 * CAPP
 PAD = 8
-BIG = 1e29
-POS = (1, 3, 7, 5)
+UW = PAD + SLOTS
+STEPS = 5
+ORDER = (0, 1, 3, 2)
+HALF = 2 * NODES
+LAND = 4 * PAIR + CAPP
 
 SCRATCH = {
     "xs": ("sbuf", [128, 4 * NODES], "bfloat16"),
     "grs": ("sbuf", [128, 4 * NODES], "bfloat16"),
+    "grp": ("sbuf", [128, 4 * NODES], "bfloat16"),
     "ws": ("sbuf", [128, 2048], "bfloat16"),
     "ws2": ("sbuf", [128, 2048], "bfloat16"),
     "snt": ("sbuf", [128, SLOTS // 16], "int32"),
-    "nbt": ("sbuf", [128, 4 * NODES // 16], "int32"),
     "ilt": ("sbuf", [128, F * NODES // 16], "int32"),
     "xg": ("sbuf", [128, 4 * SLOTS], "bfloat16"),
     "xq": ("sbuf", [128, SLOTS], "float8_e4m3fn_x4"),
@@ -22,47 +26,57 @@ SCRATCH = {
     "wp": ("sbuf", [128, 512], "uint8"),
     "vq": ("sbuf", [128, 512], "float8_e4m3fn_x4"),
     "vp": ("sbuf", [128, 512], "uint8"),
-    "landq": ("sbuf", [128, SLOTS], "float8_e4m3fn_x4"),
-    "landp": ("sbuf", [128, SLOTS], "uint8"),
-    "backq": ("sbuf", [128, SLOTS], "float8_e4m3fn_x4"),
-    "backp": ("sbuf", [128, SLOTS], "uint8"),
+    "landq": ("sbuf", [128, LAND], "float8_e4m3fn_x4"),
+    "landp": ("sbuf", [128, LAND], "uint8"),
+    "backq": ("sbuf", [128, LAND], "float8_e4m3fn_x4"),
+    "backp": ("sbuf", [128, LAND], "uint8"),
     "gs": ("sbuf", [128, 4 * SLOTS], "bfloat16"),
     "gq": ("sbuf", [128, SLOTS], "float8_e4m3fn_x4"),
     "gp": ("sbuf", [128, SLOTS], "uint8"),
     "ps": ("psum", [128, 4096], "float32"),
-    "nbl": ("sbuf", [128, 32], "uint16"),
-    "nbm": ("sbuf", [128, 32], "int32"),
-    "nbs": ("sbuf", [128, 32], "int32"),
-    "scl": ("sbuf", [128, 32], "uint16"),
+    "z": ("sbuf", [128, 4 * SLOTS], "float32"),
+    "u": ("sbuf", [128, 4 * UW], "float32"),
+    "nbd": ("dram", [4, 2, 2, 64], "int32"),
+    "nbk": ("sbuf", [128, 64], "int32"),
+    "nbl": ("sbuf", [128, 64], "uint16"),
+    "nbs": ("sbuf", [128, 16], "int32"),
+    "sc1": ("sbuf", [128, 16], "int32"),
+    "sc2": ("sbuf", [128, 16], "int32"),
+    "sc3": ("sbuf", [128, 16], "int32"),
+    "scl": ("sbuf", [128, 16], "uint16"),
     "pix": ("sbuf", [128, 1], "int32"),
     "pib": ("sbuf", [128, 1], "int32"),
     "sh": ("sbuf", [128, 1], "float32"),
-    "vals": ("sbuf", [128, 512], "float32"),
-    "win": ("sbuf", [128, 2 * SLOTS], "float32"),
-    "wint": ("sbuf", [128, 2 * SLOTS], "float32"),
-    "invf": ("sbuf", [128, 40], "float32"),
-    "inv": ("sbuf", [128, 40], "uint16"),
+    "shu": ("sbuf", [128, 1], "float32"),
+    "vals": ("sbuf", [128, HALF], "float32"),
+    "row": ("sbuf", [128, SLOTS], "float32"),
+    "parts": ("sbuf", [128, 80], "float32"),
+    "part1": ("sbuf", [128, 40], "float32"),
     "ill": ("sbuf", [128, 64], "uint16"),
-    "mpat": ("sbuf", [128, 512], "float32"),
+    "ild": ("dram", [F, 4, 4, 32], "int32"),
+    "ili": ("sbuf", [128, 128], "int32"),
+    "ilr": ("sbuf", [128, 128], "float32"),
+    "ilc": ("sbuf", [128, 128], "float32"),
+    "ilf": ("sbuf", [128, 128], "uint16"),
+    "acc0": ("sbuf", [128, HALF], "float32"),
+    "acc1": ("sbuf", [128, HALF], "float32"),
     "spat": ("sbuf", [128, 512], "float32"),
     "yt": ("sbuf", [128, 512], "float32"),
 }
 for _i in range(4):
     SCRATCH["off%d" % _i] = ("sbuf", [128, 40], "uint16")
-    SCRATCH["z%d" % _i] = ("sbuf", [128, SLOTS], "float32")
-    SCRATCH["zg%d" % _i] = ("sbuf", [128, 512], "float32")
-    SCRATCH["pm%d" % _i] = ("sbuf", [128, 512], "float32")
-    SCRATCH["grx%d" % _i] = ("sbuf", [128, 1024], "bfloat16")
-    SCRATCH["tb%d" % _i] = ("sbuf", [128, 1024], "bfloat16")
-    SCRATCH["u%d" % _i] = ("sbuf", [128, PAD + SLOTS], "float32")
 for _i in range(2):
-    SCRATCH["msk%d" % _i] = ("sbuf", [128, 1024], "bfloat16")
-for _i in range(8):
+    SCRATCH["inv%d" % _i] = ("sbuf", [128, 40], "uint16")
+    for _n in ("za", "p1", "p2", "pm"):
+        SCRATCH["%s%d" % (_n, _i)] = ("sbuf", [128, HALF], "float32")
+    for _n in ("msk", "grx", "tb"):
+        SCRATCH["%s%d" % (_n, _i)] = ("sbuf", [128, STEPS * HALF], "bfloat16")
+for _i in range(4, 8):
     SCRATCH["ug%d" % _i] = ("sbuf", [128, 512], "float32")
     SCRATCH["us%d" % _i] = ("sbuf", [128, 512], "float32")
 
-SEMAPHORES = ["sv", "ss", "st", "sg", "dsn", "dx", "dw", "dnb", "dgr", "dw2", "dil", "own1", "own2", "dy",
-              "aO", "aH", "bO", "bH", "ls"]
+SEMAPHORES = ["sv", "ss", "st", "sg", "dsn", "dx", "dw", "dnd", "dnk", "dns", "dinv", "dgr", "dw2", "dil", "did", "dii", "dy",
+              "aAB", "aC", "aD", "bAB", "bC", "bD", "ls"]
 
 
 def rank_program(g, core, T, topo):
@@ -87,292 +101,347 @@ def rank_program(g, core, T, topo):
                 queue[e].wait_ge(T.sem[name], val)
                 seen[(e, name)] = val
 
+    def copy(e, dst, src):
+        return done(e, V.tensor_copy(dst, src) if e == "v" else S.activation(dst, src, COPY))
+
     cores = list(T.cores)
-    other = [d for d in range(NR) if topo.host(cores[d]) != topo.host(core)]
-    here = [d for d in range(NR) if topo.host(cores[d]) == topo.host(core)]
-    o0, h0 = other[0] * CAPP, here[0] * CAPP
-    half = len(other) * CAPP
-    engines = {}
-    for i, d in enumerate(other):
-        e = topo.engines(core, cores[d])
-        per = len(e) // len(other)
-        engines[d] = e[i * per:(i + 1) * per]
-    chip_peer = [d for d in here if d != rank and cores[d] in topo.cores_of(core)]
-    mates = [d for d in here if d != rank and d not in chip_peer]
-    off = topo.engines(core, cores[mates[0]])
-    per = len(off) // len(mates)
-    for i, d in enumerate(mates):
-        engines[d] = off[i * per:(i + 1) * per]
-    for d in chip_peer:
-        engines[d] = [e for e in topo.engines(core, cores[d]) if e not in off][:per]
-    near = chip_peer + mates
-    inc_o = 2 * sum(len(engines[d]) for d in other)
-    inc_h = 2 * sum(len(engines[d]) for d in near)
 
-    def send(dests, sq, sp, dq, dp, sem):
-        for src, dst, codes in ((sq, dq, True), (sp, dp, False)):
-            tr = []
-            for d in dests:
-                rid, pid = topo.addr(cores[d], core)
-                a = T[src][:, d * CAPP:(d + 1) * CAPP]
-                b = T[dst][:, rank * CAPP:(rank + 1) * CAPP]
-                if codes:
-                    a, b = a.bitcast(dt.uint8), b.bitcast(dt.uint8)
-                tr.append(RemoteDMATransfer(dst_ids=[DstId(rid=rid, pnc=pid)],
-                                            dma_engine_mask=sum(1 << e for e in engines[d]),
-                                            remote_sem=T.sem[sem], src=a, dst=b))
-            g.remote_dma_fused(tr, local_sem=T.sem.ls)
+    def kinds(r):
+        c = cores[r]
+        k = {"A": [], "B": [], "C": [], "D": []}
+        for d in range(NR):
+            if cores[d] in topo.cores_of(c):
+                k["D"].append(d)
+            elif topo.mates(c, cores[d]):
+                k["C"].append(d)
+            elif topo.same_plane(c, cores[d]):
+                k["B"].append(d)
+            else:
+                k["A"].append(d)
+        return k
 
-    def keep(sq, sp, dq, dp, sem):
-        a, b = rank * CAPP, (rank + 1) * CAPP
-        Y.dma_start(out=T[dq][:, a:b].bitcast(dt.uint8), in_=T[sq][:, a:b].bitcast(dt.uint8)).then_inc(T.sem[sem], 16)
-        Y.dma_start(out=T[dp][:, a:b], in_=T[sp][:, a:b]).then_inc(T.sem[sem], 16)
+    def landing(d, s):
+        k = kinds(d)
+        if s in k["D"]:
+            first = d == k["D"][0]
+            return 3 * PAIR + (CAPP if s == d else (0 if first else PAIR))
+        if s in k["C"]:
+            return 2 * PAIR + (s - k["C"][0]) * CAPP
+        return (s - min(k["A"] + k["B"])) * CAPP
+
+    kind = kinds(rank)
+    at = {n: kind[n][0] * CAPP for n in "ABCD"}
+    at["O"], at["H"] = min(at["A"], at["B"]), min(at["C"], at["D"])
+    wide = {"A": PAIR, "B": PAIR, "C": PAIR, "D": PAIR, "O": 2 * PAIR, "H": 2 * PAIR}
+    peer = [d for d in kind["D"] if d != rank][0]
+    made = landing(rank, rank) - (rank - kind["D"][0]) * CAPP
+    off_chip = topo.engines(core, cores[kind["C"][0]])
+    on_chip = [e for e in topo.engines(core, cores[peer]) if e not in off_chip][::2]
+    n_off, n_on = len(off_chip), len(on_chip)
+    inc = {"AB": 3 * n_off, "C": 2 * n_off, "D": 2 * n_on}
+    sent = [0]
+
+    def send(dests, codes, src, dst, sem):
+        far = [d for d in dests if d != peer]
+        tr = []
+        for d in dests:
+            if d == peer:
+                eng, a0, a, name = on_chip, made + (d - kind["D"][0]) * CAPP, T[dst], "D"
+            else:
+                per = n_off // len(far)
+                eng = off_chip[far.index(d) * per:(far.index(d) + 1) * per]
+                a0, a, name = d * CAPP, T[src], "C" if d in kind["C"] else "AB"
+            b0 = landing(d, rank)
+            a, b = a[:, a0:a0 + CAPP], T[dst][:, b0:b0 + CAPP]
+            if codes:
+                a, b = a.bitcast(dt.uint8), b.bitcast(dt.uint8)
+            rid, pid = topo.addr(cores[d], core)
+            tr.append(RemoteDMATransfer(dst_ids=[DstId(rid=rid, pnc=pid)], dma_engine_mask=sum(1 << e for e in eng),
+                                        remote_sem=T.sem[sem + name], src=a, dst=b))
+            sent[0] += len(eng)
+        g.remote_dma_fused(tr, local_sem=T.sem.ls)
+
+    def quantise(q, p, t, a, n, to=None):
+        to = a if to is None else to
+        return done("v", V.quantize_mx(T[q][:, to:to + n], T[p][:, to:to + n], T[t][:, 4 * a:4 * (a + n)]))
+
+    def pack_and_send(n, tile, q, p, lq, lp, sem):
+        if n == "D":
+            need("g", quantise(lq, lp, tile, at[n], PAIR, made))
+            send(kind["C"] + [peer], True, q, lq, sem)
+            send(kind["C"] + [peer], False, p, lp, sem)
+            return
+        tok = quantise(q, p, tile, at[n], PAIR)
+        if n != "C":
+            need("g", tok)
+            send(kind[n], True, q, lq, sem)
+        if n == "B":
+            send(kind["A"] + kind["B"], False, p, lp, sem)
 
     Y.dma_start(out=T.xs[:], in_=T.x[:]).then_inc(T.sem.dx, 16)
-    for k in range(4):
-        S.dma_start(out=T.snt[16 * k:16 * k + 16, :], in_=T.sn[:, :]).then_inc(T.sem.dsn, 16)
-    for k in range(4, 8):
-        Y.dma_start(out=T.snt[16 * k:16 * k + 16, :], in_=T.sn[:, :]).then_inc(T.sem.dsn, 16)
-    S.dma_start(out=T.ws[:], in_=T.w[:]).then_inc(T.sem.dw, 16)
     for k in range(8):
-        Y.dma_start(out=T.nbt[16 * k:16 * k + 16, :], in_=T.nb[:, :]).then_inc(T.sem.dnb, 16)
-    Y.dma_start(out=T.grs[:], in_=T.gr[:]).then_inc(T.sem.dgr, 16)
-    Y.dma_start(out=T.ws2[:], in_=T.w2[:]).then_inc(T.sem.dw2, 16)
-    for k in range(8):
-        Y.dma_start(out=T.ilt[16 * k:16 * k + 16, :], in_=T.il[:, :]).then_inc(T.sem.dil, 16)
-
+        (S if k < 4 else Y).dma_start(out=T.snt[16 * k:16 * k + 16, :], in_=T.sn[:, :]).then_inc(T.sem.dsn, 16)
+    for e in range(2):
+        for i in range(2):
+            Y.dma_start(out=T.nbd[:, e, i, :], in_=T.nb[:, 16 * e:16 * e + 16]).then_inc(T.sem.dnd, 16)
     pix = done("g", g.iota(T.pix[:], [[0, 1]], 0, 1))
+    need("y", done("g", g.iota(T.nbs[:], [[16, 16]], 0, 1)))
     for k in range(4):
-        vals = done("g", g.iota(T.vals[:, k:512:4], [[8, 128]], POS[k], 0, allow_small_or_imprecise_dtypes=True))
-    mk = [None, None]
-    mk[0] = done("g", g.iota(T.msk0[:, 0:1024:2], [[0, 256], [-1, 2]], 0, 0, allow_small_or_imprecise_dtypes=True))
+        p0, c0 = 64 * (k // 2), 8 * (k % 2)
+        Y.dma_start(out=T.nbs[p0:p0 + 16, c0:c0 + 8], in_=T.nb[ORDER[k]:16:4, :]).then_inc(T.sem.dns, 16)
+    need("y", ("dx", 16))
+    Y.dma_start(out=T.ws[:], in_=T.w[:]).then_inc(T.sem.dw, 16)
+    Y.dma_start(out=T.grs[:], in_=T.gr[:]).then_inc(T.sem.dgr, 16)
+    need("y", ("dnd", 64))
+    for k in range(8):
+        Y.dma_start(out=T.nbk[16 * k:16 * k + 16, :], in_=T.nbd[:]).then_inc(T.sem.dnk, 16)
 
-    t0 = done("v", V.memset(T.mpat[:], BIG))
-    grz = [None] * 4
-    for b in (2, 3):
-        need("s", t0)
-        grz[b] = done("s", S.activation(T["grx%d" % b][:, 1:1024:2], T.mpat[:], COPY, scale=0.0))
-    win = done("v", V.memset(T.win[:], 0.0))
-    for b in (0, 1):
-        grz[b] = done("v", V.memset(T["grx%d" % b][:, 1:1024:2], 0.0))
-    need("v", t0, *[grz[b] for b in (2, 3)])
-    mpat = done("v", V.memset(T.mpat[:, 0:512:4], -BIG))
+    for k in range(2):
+        need("g", ("sg", count["g"]))
+        vals = done("g", g.iota(T.vals[64 * k:64 * k + 64, :], [[1, 2], [2 * STEPS, 64], [SLOTS, 2]], 2 * k, 0,
+                                allow_small_or_imprecise_dtypes=True))
+    done("v", V.memset(T.row[:], 0.0))
+    for h in range(2):
+        for n in ("msk", "grx"):
+            done("v", V.memset(T["%s%d" % (n, h)][:, STEPS - 1:STEPS * HALF:STEPS], 0.0))
+    need("v", pix)
+    need("v", done("v", V.tensor_scalar(T.pib[:], T.pix[:], 1, None, A.bitwise_and)))
+    done("v", V.tensor_scalar(T.sh[:], T.pib[:], float(SLOTS), None, A.mult))
+    done("v", V.tensor_scalar(T.shu[:], T.pib[:], float(UW), float(PAD), A.mult, A.add))
 
     need("v", ("dsn", 128))
     offs = {}
-    for t in (2, 0, 1, 3):
+    for t in (2, 0, 3, 1):
         offs[t] = done("v", V.tensor_scalar(T["off%d" % t][:], T.snt[:], 4.0, float(t), A.mult, A.add))
     for e in ("v", "s"):
         need(e, ("dx", 16))
-    n16 = half // 16
 
-    def gather_x(a):
-        toks = []
-        for e, t in (("v", 0), ("s", 2), ("v", 1), ("s", 3)):
-            need(e, offs[t])
-            src = T.xs[:, :].indirect(T["off%d" % t][:, a // 16:a // 16 + n16])
-            dst = T.xg[:, 4 * a + t:4 * (a + half):4]
-            toks.append(done(e, V.tensor_copy(dst, src) if e == "v" else S.activation(dst, src, COPY)))
-        return toks
+    def gather_x(e, t, n):
+        a, w = at[n], wide[n]
+        need(e, offs[t])
+        return copy(e, T.xg[:, 4 * a + t:4 * (a + w):4], T.xs[:, :].indirect(T["off%d" % t][:, a // 16:(a + w) // 16]))
 
-    def quantise(q, p, t, a, n):
-        return done("v", V.quantize_mx(T[q][:, a:a + n], T[p][:, a:a + n], T[t][:, 4 * a:4 * (a + n)]))
+    def send_x(n, *toks):
+        need("v", *toks)
+        pack_and_send(n, "xg", "xq", "xp", "landq", "landp", "a")
 
-    need("v", *gather_x(o0))
-    tok = quantise("xq", "xp", "xg", o0, half)
-    need("g", tok)
-    send(other, "xq", "xp", "landq", "landp", "aO")
-    need("v", *gather_x(h0))
-    tok = quantise("xq", "xp", "xg", h0, half)
-    need("g", tok)
-    send(near, "xq", "xp", "landq", "landp", "aH")
-    need("y", tok)
-    keep("xq", "xp", "landq", "landp", "own1")
-    mk[1] = done("g", g.iota(T.msk1[:, 0:1024:2], [[0, 256], [-1, 2]], 0, 0, allow_small_or_imprecise_dtypes=True))
+    for n in "AB":
+        send_x(n, gather_x("v", 0, n), gather_x("s", 2, n), gather_x("v", 1, n), gather_x("s", 3, n))
+    toks = [gather_x("v", 0, "H"), gather_x("s", 2, "H"), gather_x("v", 1, "C"), gather_x("s", 3, "H")]
+    last = gather_x("s", 1, "D")
+    send_x("C", *toks)
+    send_x("D", last)
 
+    need("v", ("dns", 64), vals)
+    t1 = done("v", V.tensor_scalar(T.sc1[:], T.nbs[:], 15, None, A.bitwise_and))
+    need("v", t1)
+    t1 = done("v", V.tensor_scalar(T.sc2[:], T.sc1[:], float(SLOTS - 1), None, A.mult))
+    need("v", t1)
+    t1 = done("v", V.tensor_tensor(T.sc3[:], T.sc2[:], T.nbs[:], A.add))
+    need("v", t1)
+    t1 = done("v", V.tensor_scalar(T.scl[:], T.sc3[:], 1.0 / 16, None, A.mult))
+    need("v", ("dnk", 128))
+    nbl = done("v", V.tensor_scalar(T.nbl[:], T.nbk[:], T.sh[:], None, A.add))
+    need("v", t1)
+    t1 = done("v", V.tensor_copy(T.row[:].indirect(T.scl[:]), T.vals[:]))
+    need("y", t1)
+    for k in range(2):
+        Y.dma_start(out=T.parts[:, 40 * k:40 * k + 40], in_=T.row[64 * k:64 * k + 8, :]).then_inc(T.sem.dinv, 16)
     need("v", ("dw", 16))
     wq = quantise("wq", "wp", "ws", 0, 512)
-    need("v", ("dnb", 128), pix)
-    a1 = done("v", V.tensor_scalar(T.pib[:], T.pix[:], 16, None, A.bitwise_and))
-    a2 = done("v", V.tensor_scalar(T.nbm[:], T.nbt[:], 1008, None, A.bitwise_and))
-    nbl = done("v", V.tensor_copy(T.nbl[:], T.nbt[:]))
-    need("v", a1)
-    a3 = done("v", V.tensor_copy(T.sh[:], T.pib[:]))
-    need("v", a2)
-    a4 = done("v", V.tensor_tensor(T.nbs[:], T.nbm[:], T.nbt[:], A.add))
-    need("v", a3, a4)
-    a5 = done("v", V.tensor_scalar(T.scl[:], T.nbs[:], T.sh[:], None, A.add))
-    need("v", a5, vals, win)
-    a6 = done("v", V.tensor_copy(T.win[:].indirect(T.scl[:]), T.vals[:]))
-    need("v", a6)
-    a7 = done("v", V.transpose(T.wint[:], T.win[:]))
-    need("v", a7)
-    a8 = done("v", V.tensor_tensor(T.invf[:], T.wint[:, 0:1280:32], T.wint[:, 16:1280:32], A.add))
-    need("v", a8)
-    inv = done("v", V.tensor_copy(T.inv[:], T.invf[:]))
 
     need("s", ("dgr", 16))
-    grx = [None] * 4
-    for b in range(4):
+    grp, grx = [None, None], [None, None]
+    for h in range(2):
+        for e in range(2):
+            for i in range(2):
+                grp[h] = copy("s", T.grp[:, HALF * h + 2 * e + i:HALF * (h + 1):4], T.grs[:, HALF * e + 2 * h + i:HALF * (e + 1):4])
+
+    def spread_gr(h):
+        need("s", grp[h])
         for k in range(4):
-            grx[b] = done("s", S.activation(T["grx%d" % b][:, 2 * k:1024:8], T.grs[:, b:512:4], COPY))
+            grx[h] = copy("s", T["grx%d" % h][:, k:STEPS * HALF:STEPS], T.grp[:, HALF * h:HALF * (h + 1)])
 
-    def products(stat, plane, rq, rp, a, bank, free):
-        toks = []
-        for b in range(4):
-            need("t", *free[b])
-            toks.append(done("t", P.matmul_mx(T.ps[:, 512 * (bank + b):512 * (bank + b) + half],
-                                              T[stat][:, 128 * b:128 * b + 128], T[plane][:, 128 * b:128 * b + 128],
-                                              T[rq][:, a:a + half], T[rp][:, a:a + half], True, True)))
-        return toks
+    spread_gr(0)
 
-    def unload(e, name, b, a, shift, bank, tok):
-        need(e, tok)
-        dst = T["%s%d" % (name, b)][:, shift + a:shift + a + half]
-        src = T.ps[:, 512 * (bank + b):512 * (bank + b) + half]
-        return done(e, V.tensor_copy(dst, src) if e == "v" else S.activation(dst, src, COPY))
+    col = {"O": 0, "C": 2 * PAIR, "D": min(landing(rank, rank), landing(rank, peer))}
+    arrival = {"O": "AB", "C": "C", "D": "D"}
+    emptied = []
 
-    none = [()] * 4
-    need("t", wq, ("aO", inc_o))
-    pt = products("wq", "wp", "landq", "landp", o0, 0, none)
-    zo = [None] * 4
-    for b in range(4):
-        zo[b] = unload("s" if b % 2 else "v", "z", b, o0, 0, 0, pt[b])
-    need("t", ("aH", inc_h), ("own1", 32))
-    pt = products("wq", "wp", "landq", "landp", h0, 4, none)
-    zh = [None] * 4
-    for b in (0, 1, 2, 3):
-        zh[b] = unload("s" if b == 1 else "v", "z", b, h0, 0, 4, pt[b])
+    def product(e, n, b, stat, plane, rq, rp, sem, buf, first):
+        o, a, w = 512 * (len(emptied) % 8), col[n], wide[n]
+        need("t", (sem + arrival[n], inc[arrival[n]]), *emptied[-8:-7])
+        need(e, done("t", P.matmul_mx(T.ps[:, o:o + w], T[stat][:, 128 * b:128 * b + 128], T[plane][:, 128 * b:128 * b + 128],
+                                      T[rq][:, a:a + w], T[rp][:, a:a + w], True, True)))
+        a = first + at[n]
+        if n == "D":
+            copy(e, buf[:, a:a + CAPP], T.ps[:, o + CAPP:o + PAIR])
+            emptied.append(copy(e, buf[:, a + CAPP:a + PAIR], T.ps[:, o:o + CAPP]))
+        else:
+            emptied.append(copy(e, buf[:, a:a + w], T.ps[:, o:o + w]))
+        return emptied[-1]
 
-    zg, sg = [None] * 4, {}
+    zs, inv = [[], [], [], []], [None, None]
 
-    def order_z(b):
-        need("s", zo[b], zh[b], nbl)
-        zg[b] = done("s", S.activation(T["zg%d" % b][:], T["z%d" % b][:].indirect(T.nbl[:]), COPY))
+    def z_of(*items):
+        for e, n, b in items:
+            zs[int(b)].append(product(e, n, int(b), "wq", "wp", "landq", "landp", "a", T.z, SLOTS * int(b)))
 
-    def slots(e, b, a, n):
-        need(e, inv, chain[b])
-        dst = T.gs[:, 4 * a + b:4 * (a + n):4]
-        src = T["tb%d" % b][:].indirect(T.inv[:, a // 16:(a + n) // 16])
-        return done(e, V.tensor_copy(dst, src) if e == "v" else S.activation(dst, src, COPY))
+    need("t", wq)
+    z_of("vO0", "sO1", "vD0", "sD1")
+    need("v", ("dinv", 32))
+    t2 = done("v", V.tensor_tensor(T.part1[:], T.parts[:, 0:40], T.parts[:, 40:80], A.add))
+    need("v", t2)
+    for i in range(2):
+        inv[i] = done("v", V.tensor_scalar(T["inv%d" % i][:], T.part1[:], float(STEPS * i), None, A.add))
+    z_of("vC0", "sC1", "sO2", "sO3", "sD2", "sD3", "sC2", "sC3")
 
-    pm, cm, chain = [None] * 4, [None] * 4, [None] * 4
+    need("y", ("aC", inc["C"]))
+    Y.dma_start(out=T.ws2[:], in_=T.w2[:]).then_inc(T.sem.dw2, 16)
+    for k in range(8):
+        Y.dma_start(out=T.ilt[16 * k:16 * k + 16, :], in_=T.il[:, :]).then_inc(T.sem.dil, 16)
+    for a in range(2):
+        for i in range(2):
+            for d in range(2):
+                Y.dma_start(out=T.ild[:, 2 * a + i, :, 16 * d:16 * d + 16], in_=T.il[F * a:F * a + F, :]).then_inc(T.sem.did, 16)
+    need("y", ("did", 128))
+    for k in range(4):
+        Y.dma_start(out=T.ili[32 * k:32 * k + 32, :], in_=T.ild[:]).then_inc(T.sem.dii, 16)
 
-    def running(b):
-        need("v", zg[b], mpat)
-        pm[b] = done("v", V.tensor_tensor_scan(T["pm%d" % b][:], T.mpat[:], T["zg%d" % b][:], 0.0, A.min, A.max))
+    tok = {}
 
-    def compare(b):
-        need("v", pm[b], mk[b % 2])
-        m, k = T["pm%d" % b], T["msk%d" % (b % 2)]
-        cm[b] = done("v", V.tensor_tensor(k[:, 3:1024:8], m[:, 1:512:4], m[:, 3:512:4], A.is_ge))
-        done("v", V.tensor_tensor(k[:, 1:1024:8], m[:, 0:512:4], m[:, 3:512:4], A.is_ge))
-        done("v", V.tensor_tensor(k[:, 5:1024:8], m[:, 2:512:4], m[:, 3:512:4], A.is_lt))
-        need("v", cm[b])
-        cm[b] = done("v", V.tensor_scalar(k[:, 7:1024:8], k[:, 3:1024:8], -1.0, 1.0, A.mult, A.add))
+    def zk(h, k):
+        return T.z[:, 2 * SLOTS * h:2 * SLOTS * (h + 1)].indirect(T.nbl[:, 16 * k:16 * k + 16])
 
-    def masked(b):
-        need("v", cm[b], grx[b], grz[b])
-        chain[b] = done("v", V.tensor_tensor_scan(T["tb%d" % b][:], T["msk%d" % (b % 2)][:], T["grx%d" % b][:], 0.0, A.mult, A.add))
+    def step(n, h):
+        za, p1, p2, pm, msk = (T["%s%d" % (x, h)] for x in ("za", "p1", "p2", "pm", "msk"))
+        mask = lambda k: msk[:, k:STEPS * HALF:STEPS]
+        after, call = {
+            "p1": ("za", lambda: V.tensor_tensor(p1[:], zk(h, 1), za[:], A.max)),
+            "p2": ("p1", lambda: V.tensor_tensor(p2[:], zk(h, 2), p1[:], A.max)),
+            "m": ("p2", lambda: V.tensor_tensor(pm[:], zk(h, 3), p2[:], A.max)),
+            "n2": ("p2", lambda: V.tensor_tensor(mask(2), zk(h, 3), p2[:], A.is_gt)),
+            "r1": ("m", lambda: V.tensor_tensor(mask(1), p1[:], pm[:], A.is_ge)),
+            "r0": ("m", lambda: V.tensor_tensor(mask(0), zk(h, 0), pm[:], A.is_ge)),
+            "n1": ("r1", lambda: V.tensor_scalar(mask(3), mask(1), -1.0, 1.0, A.mult, A.add)),
+            "scan": ("n1", lambda: V.tensor_tensor_scan(T["tb%d" % h][:], T["grx%d" % h][:], msk[:], 0.0, A.subtract, A.mult)),
+        }[n]
+        need("v", tok[after, h])
+        if n == "scan":
+            need("v", grx[h], tok["r0", h], tok["n2", h])
+        tok[n, h] = done("v", call())
 
-    order_z(0)
-    order_z(1)
-    running(0)
-    compare(0)
-    running(1)
-    masked(0)
-    order_z(2)
-    slots0 = slots("s", 0, 0, SLOTS)
-    compare(1)
-    running(2)
-    masked(1)
-    order_z(3)
-    slots1 = slots("s", 1, 0, SLOTS)
-    compare(2)
-    running(3)
-    masked(2)
-    slots2 = slots("s", 2, 0, SLOTS)
-    compare(3)
-    masked(3)
-    q1 = slots("v", 3, o0, half // 2)
-    q2 = slots("s", 3, o0 + half // 2, half // 2)
-    q3 = slots("s", 3, h0, half)
-    need("v", q1, slots0, slots1, slots2, q2)
-    tok = quantise("gq", "gp", "gs", o0, half)
-    need("g", tok)
-    send(other, "gq", "gp", "backq", "backp", "bO")
-    need("v", q3)
-    tok = quantise("gq", "gp", "gs", h0, half)
-    need("g", tok)
-    send(near, "gq", "gp", "backq", "backp", "bH")
-    need("y", tok)
-    keep("gq", "gp", "backq", "backp", "own2")
+    def first(e, h):
+        need(e, nbl, *(zs[2 * h] + zs[2 * h + 1]))
+        tok["za", h] = copy(e, T["za%d" % h][:], zk(h, 0))
+
+    def slots(e, b, n):
+        a, w = at[n], wide[n]
+        need(e, inv[b % 2], tok["scan", b // 2])
+        return copy(e, T.gs[:, 4 * a + b:4 * (a + w):4], T["tb%d" % (b // 2)][:].indirect(T["inv%d" % (b % 2)][:, a // 16:(a + w) // 16]))
+
+    first("v", 0)
+    first("s", 1)
+    spread_gr(1)
+    for n, h in (("p1", 0), ("p2", 0), ("m", 0), ("n2", 0), ("r1", 0), ("r0", 0), ("n1", 0), ("p1", 1), ("scan", 0),
+                 ("p2", 1), ("m", 1), ("n2", 1), ("r1", 1), ("r0", 1), ("n1", 1), ("scan", 1)):
+        step(n, h)
+    early = {n: [slots("s", b, n) for b in (0, 1)] for n in "OH"}
+
+    def send_g(n, *toks):
+        need("v", *toks)
+        pack_and_send(n, "gs", "gq", "gp", "backq", "backp", "b")
+
+    for n in "AB":
+        send_g(n, slots("v", 2, n), slots("s", 3, n), *early["O"])
+    toks = [slots("v", 2, "C"), slots("s", 3, "H")] + early["H"]
+    last = slots("s", 2, "D")
+    send_g("C", *toks)
+    send_g("D", last)
 
     need("v", ("dw2", 16))
     vq = quantise("vq", "vp", "ws2", 0, 512)
     need("v", ("dil", 128))
     ill = done("v", V.tensor_scalar(T.ill[:], T.ilt[:], float(PAD), None, A.add))
-    zpad = [done("v", V.memset(T["u%d" % b][:, 0:PAD], 0.0)) for b in range(4)]
-    c1 = done("v", V.memset(T.spat[:], 1.0))
-    need("v", c1)
-    spat = done("v", V.memset(T.spat[:, 0:512:8], 0.0))
-
-    need("t", vq, ("bO", inc_o))
-    pt = products("vq", "vp", "backq", "backp", o0, 0, [(zo[b],) for b in range(4)])
-    uo = [None] * 4
     for b in range(4):
-        uo[b] = unload("s" if b % 2 else "v", "u", b, o0, PAD, 0, pt[b])
-    need("t", ("bH", inc_h), ("own2", 32))
-    pt = products("vq", "vp", "backq", "backp", h0, 4, [(zh[b],) for b in range(4)])
-    uh = [None] * 4
-    for b in range(4):
-        uh[b] = unload("s" if b == 1 else "v", "u", b, h0, PAD, 4, pt[b])
+        done("v", V.memset(T.u[:, UW * b:UW * b + PAD], 0.0))
+    need("v", done("v", V.memset(T.spat[:], 1.0)))
+    need("v", ("dii", 64))
+    t3 = done("v", V.tensor_scalar(T.ilr[:], T.ili[:], T.shu[:], None, A.add))
+    spat = done("v", V.memset(T.spat[:, 0:512:F], 0.0))
+    need("v", t3)
+    need("v", done("v", V.transpose(T.ilc[:], T.ilr[:])))
+    for c in range(4):
+        ilf = done("v", V.tensor_copy(T.ilf[:, c:128:4], T.ilc[:, 32 * c:32 * c + 32]))
 
-    ug, us, yt = [None] * 8, [None] * 8, [None] * 8
+    uu = [[], [], [], []]
 
-    def take(e, i):
-        b, h = i // 2, i % 2
-        need(e, uo[b], uh[b], zpad[b], ill)
-        src = T["u%d" % b][:].indirect(T.ill[:, 32 * h:32 * h + 32])
-        dst = T["ug%d" % i][:]
-        ug[i] = done(e, V.tensor_copy(dst, src) if e == "v" else S.activation(dst, src, COPY))
+    def u_of(*items):
+        for e, n, b in items:
+            uu[int(b)].append(product(e, n, int(b), "vq", "vp", "backq", "backp", "b", T.u, UW * int(b) + PAD))
 
-    def add_up(i):
-        need("v", ug[i], spat)
-        us[i] = done("v", V.tensor_tensor_scan(T["us%d" % i][:], T.spat[:], T["ug%d" % i][:], 0.0, A.mult, A.add))
+    acc = [None]
 
-    def pick(i):
-        need("v", us[i])
-        yt[i] = done("v", V.tensor_copy(T.yt[:, 64 * i:64 * i + 64], T["us%d" % i][:, 7:512:8]))
+    def gather_add(f):
+        old, new = T["acc%d" % ((f + 1) % 2)], T["acc%d" % (f % 2)]
+        src = lambda a, n: T.u[:, 0:2 * UW].indirect(T.ilf[:, 16 * f + a:16 * f + a + n])
+        if f == 0:
+            need("v", ilf, *(uu[0] + uu[1]))
+            acc[0] = copy("v", new[:], src(0, 16))
+            return
+        need("v", acc[0])
+        if f < F - 1:
+            acc[0] = done("v", V.tensor_tensor(new[:], src(0, 16), old[:], A.add))
+            return
+        for a in range(2):
+            acc[0] = done("v", V.tensor_tensor(T.yt[:, a:HALF:2], src(8 * a, 8), old[:, NODES * a:NODES * (a + 1)], A.add))
 
-    def store(b):
-        need("y", yt[2 * b], yt[2 * b + 1])
-        Y.dma_start(out=T.y[:, 128 * b:128 * b + 128], in_=T.yt[:, 128 * b:128 * b + 128]).then_inc(T.sem.dy, 16)
+    ug, us = {}, {}
 
-    for i in range(7):
-        take("s", i)
-    add_up(0)
-    add_up(1)
-    pick(0)
-    pick(1)
-    add_up(2)
-    store(0)
-    take("v", 7)
-    add_up(3)
-    pick(2)
-    pick(3)
-    store(1)
-    add_up(4)
-    add_up(5)
-    pick(4)
-    pick(5)
-    store(2)
-    add_up(7)
-    add_up(6)
-    pick(7)
-    pick(6)
-    store(3)
+    def take(e, b, a, n):
+        need(e, spat, *uu[b])
+        buf = T["ug%d" % (2 * b + a // 64)][:, F * (a % 64):F * (a % 64 + n)]
+        ug[b, a] = copy(e, buf, T.u[:, UW * b:UW * (b + 1)].indirect(T.ill[:, a // 2:(a + n) // 2]))
 
-    Y.wait_ge(T.sem.dy, 64)
+    def add_up(b, a, n):
+        need("v", ug[b, a])
+        i, c = 2 * b + a // 64, slice(F * (a % 64), F * (a % 64 + n))
+        us[b, a] = done("v", V.tensor_tensor_scan(T["us%d" % i][:, c], T.spat[:, c], T["ug%d" % i][:, c], 0.0, A.mult, A.add))
+
+    def pick(e, b, a, *parts):
+        need(e, *[us[b, p] for p in parts])
+        src, dst = T["us%d" % (2 * b + a // 64)][:, F - 1:512:F], T.yt[:, NODES * b + a:NODES * b + a + 64]
+        if e == "g":
+            return done(e, g.affine_select(dst, src, [[0, 64]], A.is_ge, 0.0, 0, 0))
+        return copy(e, dst, src)
+
+    stores = [0]
+
+    def store(a, n, *toks):
+        need("y", *toks)
+        Y.dma_start(out=T.y[:, a:a + n], in_=T.yt[:, a:a + n]).then_inc(T.sem.dy, 16)
+        stores[0] += 16
+
+    need("t", vq)
+    u_of("vO0", "sO1", "vD0", "sD1", "vC0", "sC1", "sO2", "sD2", "sC2")
+    take("s", 2, 0, 64)
+    u_of("sO3", "sD3", "sC3")
+    for b, a in ((2, 64), (3, 0), (3, 64)):
+        take("s", b, a, 64)
+    for f in range(5):
+        gather_add(f)
+    add_up(2, 0, 64)
+    gather_add(5)
+    add_up(2, 64, 64)
+    gather_add(6)
+    add_up(3, 0, 64)
+    picked = [pick("g", b, a, a) for b, a in ((2, 0), (2, 64), (3, 0))]
+    add_up(3, 64, 64)
+    gather_add(7)
+    store(HALF, NODES, *picked[0:2])
+    store(HALF + NODES, NODES, picked[2], pick("s", 3, 64, 64))
+    store(0, HALF, acc[0])
+
+    Y.wait_ge(T.sem.dy, stores[0])
     need("g", ("sv", count["v"]), ("ss", count["s"]), ("st", count["t"]), ("sg", count["g"]))
-    g.wait_ge(T.sem.ls, 2 * (inc_o + inc_h))
+    g.wait_ge(T.sem.ls, sent[0])

from concourse.bass import DstId, RemoteDMATransfer
from concourse.mybir import dt, AluOpType, ActivationFunctionType

NR, NODES, CAPP, F = 8, 128, 80, 8
SLOTS = NR * CAPP
PAIR = 2 * CAPP
PAD = 8
UW = PAD + SLOTS
STEPS = 5
ORDER = (0, 1, 3, 2)
HALF = 2 * NODES
LAND = 4 * PAIR + CAPP

SCRATCH = {
    "xs": ("sbuf", [128, 4 * NODES], "bfloat16"),
    "grs": ("sbuf", [128, 4 * NODES], "bfloat16"),
    "grp": ("sbuf", [128, 4 * NODES], "bfloat16"),
    "ws": ("sbuf", [128, 2048], "bfloat16"),
    "ws2": ("sbuf", [128, 2048], "bfloat16"),
    "snt": ("sbuf", [128, SLOTS // 16], "int32"),
    "ilt": ("sbuf", [128, F * NODES // 16], "int32"),
    "xg": ("sbuf", [128, 4 * SLOTS], "bfloat16"),
    "xq": ("sbuf", [128, SLOTS], "float8_e4m3fn_x4"),
    "xp": ("sbuf", [128, SLOTS], "uint8"),
    "wq": ("sbuf", [128, 512], "float8_e4m3fn_x4"),
    "wp": ("sbuf", [128, 512], "uint8"),
    "vq": ("sbuf", [128, 512], "float8_e4m3fn_x4"),
    "vp": ("sbuf", [128, 512], "uint8"),
    "landq": ("sbuf", [128, LAND], "float8_e4m3fn_x4"),
    "landp": ("sbuf", [128, LAND], "uint8"),
    "backq": ("sbuf", [128, LAND], "float8_e4m3fn_x4"),
    "backp": ("sbuf", [128, LAND], "uint8"),
    "gs": ("sbuf", [128, 4 * SLOTS], "bfloat16"),
    "gq": ("sbuf", [128, SLOTS], "float8_e4m3fn_x4"),
    "gp": ("sbuf", [128, SLOTS], "uint8"),
    "ps": ("psum", [128, 4096], "float32"),
    "z": ("sbuf", [128, 4 * SLOTS], "float32"),
    "u": ("sbuf", [128, 4 * UW], "float32"),
    "nbd": ("dram", [4, 2, 2, 64], "int32"),
    "nbk": ("sbuf", [128, 64], "int32"),
    "nbl": ("sbuf", [128, 64], "uint16"),
    "nbs": ("sbuf", [128, 16], "int32"),
    "sc1": ("sbuf", [128, 16], "int32"),
    "sc2": ("sbuf", [128, 16], "int32"),
    "sc3": ("sbuf", [128, 16], "int32"),
    "scl": ("sbuf", [128, 16], "uint16"),
    "pix": ("sbuf", [128, 1], "int32"),
    "pib": ("sbuf", [128, 1], "int32"),
    "sh": ("sbuf", [128, 1], "float32"),
    "shu": ("sbuf", [128, 1], "float32"),
    "vals": ("sbuf", [128, HALF], "float32"),
    "row": ("sbuf", [128, SLOTS], "float32"),
    "parts": ("sbuf", [128, 80], "float32"),
    "part1": ("sbuf", [128, 40], "float32"),
    "ill": ("sbuf", [128, 64], "uint16"),
    "ild": ("dram", [F, 4, 4, 32], "int32"),
    "ili": ("sbuf", [128, 128], "int32"),
    "ilr": ("sbuf", [128, 128], "float32"),
    "ilc": ("sbuf", [128, 128], "float32"),
    "ilf": ("sbuf", [128, 128], "uint16"),
    "acc0": ("sbuf", [128, HALF], "float32"),
    "acc1": ("sbuf", [128, HALF], "float32"),
    "spat": ("sbuf", [128, 512], "float32"),
    "yt": ("sbuf", [128, 512], "float32"),
}
for _i in range(4):
    SCRATCH["off%d" % _i] = ("sbuf", [128, 40], "uint16")
for _i in range(2):
    SCRATCH["inv%d" % _i] = ("sbuf", [128, 40], "uint16")
    for _n in ("za", "p1", "p2", "pm"):
        SCRATCH["%s%d" % (_n, _i)] = ("sbuf", [128, HALF], "float32")
    for _n in ("msk", "grx", "tb"):
        SCRATCH["%s%d" % (_n, _i)] = ("sbuf", [128, STEPS * HALF], "bfloat16")
for _i in range(4, 8):
    SCRATCH["ug%d" % _i] = ("sbuf", [128, 512], "float32")
    SCRATCH["us%d" % _i] = ("sbuf", [128, 512], "float32")

SEMAPHORES = ["sv", "ss", "st", "sg", "dsn", "dx", "dw", "dnd", "dnk", "dns", "dinv", "dgr", "dw2", "dil", "did", "dii", "dy",
              "aAB", "aC", "aD", "bAB", "bC", "bD", "ls"]


def rank_program(g, core, T, topo):
    rank = T.rank_of(core)
    if rank is None:
        return
    A, COPY = AluOpType, ActivationFunctionType.Copy
    V, S, P, Y = g.vector, g.scalar, g.tensor, g.sync
    queue = {"v": V, "s": S, "t": P, "g": g, "y": Y}
    sem_of = {"v": "sv", "s": "ss", "t": "st", "g": "sg"}
    count = {"v": 0, "s": 0, "t": 0, "g": 0}
    seen = {}

    def done(e, ins):
        ins.then_inc(T.sem[sem_of[e]], 1)
        count[e] += 1
        return (sem_of[e], count[e])

    def need(e, *tokens):
        for name, val in tokens:
            if seen.get((e, name), 0) < val:
                queue[e].wait_ge(T.sem[name], val)
                seen[(e, name)] = val

    def copy(e, dst, src):
        return done(e, V.tensor_copy(dst, src) if e == "v" else S.activation(dst, src, COPY))

    cores = list(T.cores)

    def kinds(r):
        c = cores[r]
        k = {"A": [], "B": [], "C": [], "D": []}
        for d in range(NR):
            if cores[d] in topo.cores_of(c):
                k["D"].append(d)
            elif topo.mates(c, cores[d]):
                k["C"].append(d)
            elif topo.same_plane(c, cores[d]):
                k["B"].append(d)
            else:
                k["A"].append(d)
        return k

    def landing(d, s):
        k = kinds(d)
        if s in k["D"]:
            first = d == k["D"][0]
            return 3 * PAIR + (CAPP if s == d else (0 if first else PAIR))
        if s in k["C"]:
            return 2 * PAIR + (s - k["C"][0]) * CAPP
        return (s - min(k["A"] + k["B"])) * CAPP

    kind = kinds(rank)
    at = {n: kind[n][0] * CAPP for n in "ABCD"}
    at["O"], at["H"] = min(at["A"], at["B"]), min(at["C"], at["D"])
    wide = {"A": PAIR, "B": PAIR, "C": PAIR, "D": PAIR, "O": 2 * PAIR, "H": 2 * PAIR}
    peer = [d for d in kind["D"] if d != rank][0]
    made = landing(rank, rank) - (rank - kind["D"][0]) * CAPP
    off_chip = topo.engines(core, cores[kind["C"][0]])
    on_chip = [e for e in topo.engines(core, cores[peer]) if e not in off_chip][::2]
    n_off, n_on = len(off_chip), len(on_chip)
    inc = {"AB": 3 * n_off, "C": 2 * n_off, "D": 2 * n_on}
    sent = [0]

    def send(dests, codes, src, dst, sem):
        far = [d for d in dests if d != peer]
        tr = []
        for d in dests:
            if d == peer:
                eng, a0, a, name = on_chip, made + (d - kind["D"][0]) * CAPP, T[dst], "D"
            else:
                per = n_off // len(far)
                eng = off_chip[far.index(d) * per:(far.index(d) + 1) * per]
                a0, a, name = d * CAPP, T[src], "C" if d in kind["C"] else "AB"
            b0 = landing(d, rank)
            a, b = a[:, a0:a0 + CAPP], T[dst][:, b0:b0 + CAPP]
            if codes:
                a, b = a.bitcast(dt.uint8), b.bitcast(dt.uint8)
            rid, pid = topo.addr(cores[d], core)
            tr.append(RemoteDMATransfer(dst_ids=[DstId(rid=rid, pnc=pid)], dma_engine_mask=sum(1 << e for e in eng),
                                        remote_sem=T.sem[sem + name], src=a, dst=b))
            sent[0] += len(eng)
        g.remote_dma_fused(tr, local_sem=T.sem.ls)

    def quantise(q, p, t, a, n, to=None):
        to = a if to is None else to
        return done("v", V.quantize_mx(T[q][:, to:to + n], T[p][:, to:to + n], T[t][:, 4 * a:4 * (a + n)]))

    def pack_and_send(n, tile, q, p, lq, lp, sem):
        if n == "D":
            need("g", quantise(lq, lp, tile, at[n], PAIR, made))
            send(kind["C"] + [peer], True, q, lq, sem)
            send(kind["C"] + [peer], False, p, lp, sem)
            return
        tok = quantise(q, p, tile, at[n], PAIR)
        if n != "C":
            need("g", tok)
            send(kind[n], True, q, lq, sem)
        if n == "B":
            send(kind["A"] + kind["B"], False, p, lp, sem)

    Y.dma_start(out=T.xs[:], in_=T.x[:]).then_inc(T.sem.dx, 16)
    for k in range(8):
        (S if k < 4 else Y).dma_start(out=T.snt[16 * k:16 * k + 16, :], in_=T.sn[:, :]).then_inc(T.sem.dsn, 16)
    for e in range(2):
        for i in range(2):
            Y.dma_start(out=T.nbd[:, e, i, :], in_=T.nb[:, 16 * e:16 * e + 16]).then_inc(T.sem.dnd, 16)
    pix = done("g", g.iota(T.pix[:], [[0, 1]], 0, 1))
    need("y", done("g", g.iota(T.nbs[:], [[16, 16]], 0, 1)))
    for k in range(4):
        p0, c0 = 64 * (k // 2), 8 * (k % 2)
        Y.dma_start(out=T.nbs[p0:p0 + 16, c0:c0 + 8], in_=T.nb[ORDER[k]:16:4, :]).then_inc(T.sem.dns, 16)
    need("y", ("dx", 16))
    Y.dma_start(out=T.ws[:], in_=T.w[:]).then_inc(T.sem.dw, 16)
    Y.dma_start(out=T.grs[:], in_=T.gr[:]).then_inc(T.sem.dgr, 16)
    need("y", ("dnd", 64))
    for k in range(8):
        Y.dma_start(out=T.nbk[16 * k:16 * k + 16, :], in_=T.nbd[:]).then_inc(T.sem.dnk, 16)

    for k in range(2):
        need("g", ("sg", count["g"]))
        vals = done("g", g.iota(T.vals[64 * k:64 * k + 64, :], [[1, 2], [2 * STEPS, 64], [SLOTS, 2]], 2 * k, 0,
                                allow_small_or_imprecise_dtypes=True))
    done("v", V.memset(T.row[:], 0.0))
    for h in range(2):
        for n in ("msk", "grx"):
            done("v", V.memset(T["%s%d" % (n, h)][:, STEPS - 1:STEPS * HALF:STEPS], 0.0))
    need("v", pix)
    need("v", done("v", V.tensor_scalar(T.pib[:], T.pix[:], 1, None, A.bitwise_and)))
    done("v", V.tensor_scalar(T.sh[:], T.pib[:], float(SLOTS), None, A.mult))
    done("v", V.tensor_scalar(T.shu[:], T.pib[:], float(UW), float(PAD), A.mult, A.add))

    need("v", ("dsn", 128))
    offs = {}
    for t in (2, 0, 3, 1):
        offs[t] = done("v", V.tensor_scalar(T["off%d" % t][:], T.snt[:], 4.0, float(t), A.mult, A.add))
    for e in ("v", "s"):
        need(e, ("dx", 16))

    def gather_x(e, t, n):
        a, w = at[n], wide[n]
        need(e, offs[t])
        return copy(e, T.xg[:, 4 * a + t:4 * (a + w):4], T.xs[:, :].indirect(T["off%d" % t][:, a // 16:(a + w) // 16]))

    def send_x(n, *toks):
        need("v", *toks)
        pack_and_send(n, "xg", "xq", "xp", "landq", "landp", "a")

    for n in "AB":
        send_x(n, gather_x("v", 0, n), gather_x("s", 2, n), gather_x("v", 1, n), gather_x("s", 3, n))
    toks = [gather_x("v", 0, "H"), gather_x("s", 2, "H"), gather_x("v", 1, "C"), gather_x("s", 3, "H")]
    last = gather_x("s", 1, "D")
    send_x("C", *toks)
    send_x("D", last)

    need("v", ("dns", 64), vals)
    t1 = done("v", V.tensor_scalar(T.sc1[:], T.nbs[:], 15, None, A.bitwise_and))
    need("v", t1)
    t1 = done("v", V.tensor_scalar(T.sc2[:], T.sc1[:], float(SLOTS - 1), None, A.mult))
    need("v", t1)
    t1 = done("v", V.tensor_tensor(T.sc3[:], T.sc2[:], T.nbs[:], A.add))
    need("v", t1)
    t1 = done("v", V.tensor_scalar(T.scl[:], T.sc3[:], 1.0 / 16, None, A.mult))
    need("v", ("dnk", 128))
    nbl = done("v", V.tensor_scalar(T.nbl[:], T.nbk[:], T.sh[:], None, A.add))
    need("v", t1)
    t1 = done("v", V.tensor_copy(T.row[:].indirect(T.scl[:]), T.vals[:]))
    need("y", t1)
    for k in range(2):
        Y.dma_start(out=T.parts[:, 40 * k:40 * k + 40], in_=T.row[64 * k:64 * k + 8, :]).then_inc(T.sem.dinv, 16)
    need("v", ("dw", 16))
    wq = quantise("wq", "wp", "ws", 0, 512)

    need("s", ("dgr", 16))
    grp, grx = [None, None], [None, None]
    for h in range(2):
        for e in range(2):
            for i in range(2):
                grp[h] = copy("s", T.grp[:, HALF * h + 2 * e + i:HALF * (h + 1):4], T.grs[:, HALF * e + 2 * h + i:HALF * (e + 1):4])

    def spread_gr(h):
        need("s", grp[h])
        for k in range(4):
            grx[h] = copy("s", T["grx%d" % h][:, k:STEPS * HALF:STEPS], T.grp[:, HALF * h:HALF * (h + 1)])

    spread_gr(0)

    col = {"O": 0, "C": 2 * PAIR, "D": min(landing(rank, rank), landing(rank, peer))}
    arrival = {"O": "AB", "C": "C", "D": "D"}
    emptied = []

    def product(e, n, b, stat, plane, rq, rp, sem, buf, first):
        o, a, w = 512 * (len(emptied) % 8), col[n], wide[n]
        need("t", (sem + arrival[n], inc[arrival[n]]), *emptied[-8:-7])
        need(e, done("t", P.matmul_mx(T.ps[:, o:o + w], T[stat][:, 128 * b:128 * b + 128], T[plane][:, 128 * b:128 * b + 128],
                                      T[rq][:, a:a + w], T[rp][:, a:a + w], True, True)))
        a = first + at[n]
        if n == "D":
            copy(e, buf[:, a:a + CAPP], T.ps[:, o + CAPP:o + PAIR])
            emptied.append(copy(e, buf[:, a + CAPP:a + PAIR], T.ps[:, o:o + CAPP]))
        else:
            emptied.append(copy(e, buf[:, a:a + w], T.ps[:, o:o + w]))
        return emptied[-1]

    zs, inv = [[], [], [], []], [None, None]

    def z_of(*items):
        for e, n, b in items:
            zs[int(b)].append(product(e, n, int(b), "wq", "wp", "landq", "landp", "a", T.z, SLOTS * int(b)))

    need("t", wq)
    z_of("vO0", "sO1", "vD0", "sD1")
    need("v", ("dinv", 32))
    t2 = done("v", V.tensor_tensor(T.part1[:], T.parts[:, 0:40], T.parts[:, 40:80], A.add))
    need("v", t2)
    for i in range(2):
        inv[i] = done("v", V.tensor_scalar(T["inv%d" % i][:], T.part1[:], float(STEPS * i), None, A.add))
    z_of("vC0", "sC1", "sO2", "sO3", "sD2", "sD3", "sC2", "sC3")

    need("y", ("aC", inc["C"]))
    Y.dma_start(out=T.ws2[:], in_=T.w2[:]).then_inc(T.sem.dw2, 16)
    for k in range(8):
        Y.dma_start(out=T.ilt[16 * k:16 * k + 16, :], in_=T.il[:, :]).then_inc(T.sem.dil, 16)
    for a in range(2):
        for i in range(2):
            for d in range(2):
                Y.dma_start(out=T.ild[:, 2 * a + i, :, 16 * d:16 * d + 16], in_=T.il[F * a:F * a + F, :]).then_inc(T.sem.did, 16)
    need("y", ("did", 128))
    for k in range(4):
        Y.dma_start(out=T.ili[32 * k:32 * k + 32, :], in_=T.ild[:]).then_inc(T.sem.dii, 16)

    tok = {}

    def zk(h, k):
        return T.z[:, 2 * SLOTS * h:2 * SLOTS * (h + 1)].indirect(T.nbl[:, 16 * k:16 * k + 16])

    def step(n, h):
        za, p1, p2, pm, msk = (T["%s%d" % (x, h)] for x in ("za", "p1", "p2", "pm", "msk"))
        mask = lambda k: msk[:, k:STEPS * HALF:STEPS]
        after, call = {
            "p1": ("za", lambda: V.tensor_tensor(p1[:], zk(h, 1), za[:], A.max)),
            "p2": ("p1", lambda: V.tensor_tensor(p2[:], zk(h, 2), p1[:], A.max)),
            "m": ("p2", lambda: V.tensor_tensor(pm[:], zk(h, 3), p2[:], A.max)),
            "n2": ("p2", lambda: V.tensor_tensor(mask(2), zk(h, 3), p2[:], A.is_gt)),
            "r1": ("m", lambda: V.tensor_tensor(mask(1), p1[:], pm[:], A.is_ge)),
            "r0": ("m", lambda: V.tensor_tensor(mask(0), zk(h, 0), pm[:], A.is_ge)),
            "n1": ("r1", lambda: V.tensor_scalar(mask(3), mask(1), -1.0, 1.0, A.mult, A.add)),
            "scan": ("n1", lambda: V.tensor_tensor_scan(T["tb%d" % h][:], T["grx%d" % h][:], msk[:], 0.0, A.subtract, A.mult)),
        }[n]
        need("v", tok[after, h])
        if n == "scan":
            need("v", grx[h], tok["r0", h], tok["n2", h])
        tok[n, h] = done("v", call())

    def first(e, h):
        need(e, nbl, *(zs[2 * h] + zs[2 * h + 1]))
        tok["za", h] = copy(e, T["za%d" % h][:], zk(h, 0))

    def slots(e, b, n):
        a, w = at[n], wide[n]
        need(e, inv[b % 2], tok["scan", b // 2])
        return copy(e, T.gs[:, 4 * a + b:4 * (a + w):4], T["tb%d" % (b // 2)][:].indirect(T["inv%d" % (b % 2)][:, a // 16:(a + w) // 16]))

    first("v", 0)
    first("s", 1)
    spread_gr(1)
    for n, h in (("p1", 0), ("p2", 0), ("m", 0), ("n2", 0), ("r1", 0), ("r0", 0), ("n1", 0), ("p1", 1), ("scan", 0),
                 ("p2", 1), ("m", 1), ("n2", 1), ("r1", 1), ("r0", 1), ("n1", 1), ("scan", 1)):
        step(n, h)
    early = {n: [slots("s", b, n) for b in (0, 1)] for n in "OH"}

    def send_g(n, *toks):
        need("v", *toks)
        pack_and_send(n, "gs", "gq", "gp", "backq", "backp", "b")

    for n in "AB":
        send_g(n, slots("v", 2, n), slots("s", 3, n), *early["O"])
    toks = [slots("v", 2, "C"), slots("s", 3, "H")] + early["H"]
    last = slots("s", 2, "D")
    send_g("C", *toks)
    send_g("D", last)

    need("v", ("dw2", 16))
    vq = quantise("vq", "vp", "ws2", 0, 512)
    need("v", ("dil", 128))
    ill = done("v", V.tensor_scalar(T.ill[:], T.ilt[:], float(PAD), None, A.add))
    for b in range(4):
        done("v", V.memset(T.u[:, UW * b:UW * b + PAD], 0.0))
    need("v", done("v", V.memset(T.spat[:], 1.0)))
    need("v", ("dii", 64))
    t3 = done("v", V.tensor_scalar(T.ilr[:], T.ili[:], T.shu[:], None, A.add))
    spat = done("v", V.memset(T.spat[:, 0:512:F], 0.0))
    need("v", t3)
    need("v", done("v", V.transpose(T.ilc[:], T.ilr[:])))
    for c in range(4):
        ilf = done("v", V.tensor_copy(T.ilf[:, c:128:4], T.ilc[:, 32 * c:32 * c + 32]))

    uu = [[], [], [], []]

    def u_of(*items):
        for e, n, b in items:
            uu[int(b)].append(product(e, n, int(b), "vq", "vp", "backq", "backp", "b", T.u, UW * int(b) + PAD))

    acc = [None]

    def gather_add(f):
        old, new = T["acc%d" % ((f + 1) % 2)], T["acc%d" % (f % 2)]
        src = lambda a, n: T.u[:, 0:2 * UW].indirect(T.ilf[:, 16 * f + a:16 * f + a + n])
        if f == 0:
            need("v", ilf, *(uu[0] + uu[1]))
            acc[0] = copy("v", new[:], src(0, 16))
            return
        need("v", acc[0])
        if f < F - 1:
            acc[0] = done("v", V.tensor_tensor(new[:], src(0, 16), old[:], A.add))
            return
        for a in range(2):
            acc[0] = done("v", V.tensor_tensor(T.yt[:, a:HALF:2], src(8 * a, 8), old[:, NODES * a:NODES * (a + 1)], A.add))

    ug, us = {}, {}

    def take(e, b, a, n):
        need(e, spat, *uu[b])
        buf = T["ug%d" % (2 * b + a // 64)][:, F * (a % 64):F * (a % 64 + n)]
        ug[b, a] = copy(e, buf, T.u[:, UW * b:UW * (b + 1)].indirect(T.ill[:, a // 2:(a + n) // 2]))

    def add_up(b, a, n):
        need("v", ug[b, a])
        i, c = 2 * b + a // 64, slice(F * (a % 64), F * (a % 64 + n))
        us[b, a] = done("v", V.tensor_tensor_scan(T["us%d" % i][:, c], T.spat[:, c], T["ug%d" % i][:, c], 0.0, A.mult, A.add))

    def pick(e, b, a, *parts):
        need(e, *[us[b, p] for p in parts])
        src, dst = T["us%d" % (2 * b + a // 64)][:, F - 1:512:F], T.yt[:, NODES * b + a:NODES * b + a + 64]
        if e == "g":
            return done(e, g.affine_select(dst, src, [[0, 64]], A.is_ge, 0.0, 0, 0))
        return copy(e, dst, src)

    stores = [0]

    def store(a, n, *toks):
        need("y", *toks)
        Y.dma_start(out=T.y[:, a:a + n], in_=T.yt[:, a:a + n]).then_inc(T.sem.dy, 16)
        stores[0] += 16

    need("t", vq)
    u_of("vO0", "sO1", "vD0", "sD1", "vC0", "sC1", "sO2", "sD2", "sC2")
    take("s", 2, 0, 64)
    u_of("sO3", "sD3", "sC3")
    for b, a in ((2, 64), (3, 0), (3, 64)):
        take("s", b, a, 64)
    for f in range(5):
        gather_add(f)
    add_up(2, 0, 64)
    gather_add(5)
    add_up(2, 64, 64)
    gather_add(6)
    add_up(3, 0, 64)
    picked = [pick("g", b, a, a) for b, a in ((2, 0), (2, 64), (3, 0))]
    add_up(3, 64, 64)
    gather_add(7)
    store(HALF, NODES, *picked[0:2])
    store(HALF + NODES, NODES, picked[2], pick("s", 3, 64, 64))
    store(0, HALF, acc[0])

    Y.wait_ge(T.sem.dy, stores[0])
    need("g", ("sv", count["v"]), ("ss", count["s"]), ("st", count["t"]), ("sg", count["g"]))
    g.wait_ge(T.sem.ls, sent[0])
